import numpy as np
import ml_dtypes


def mxq(x, axis, fmt="e4m3"):
    dtype, down = {"e4m3": (ml_dtypes.float8_e4m3fn, 7), "e5m2": (ml_dtypes.float8_e5m2, 14)}[fmt]
    v = np.moveaxis(np.asarray(x, np.float32).astype(ml_dtypes.bfloat16).astype(np.float64), axis, -1)
    blocks = v.reshape(v.shape[:-1] + (-1, 32))
    amax = np.abs(blocks).max(-1, keepdims=True)
    byte = np.maximum(np.where(amax > 0, np.frexp(amax)[1] - 1 + 127, 0) - down, 1)
    scale = np.exp2(byte - 127.0)
    codes = (blocks / scale).astype(np.float32).astype(dtype).astype(np.float64)
    return np.moveaxis((codes * scale).reshape(v.shape), -1, axis)


WIDE = False


def mx_kscale(k):
    if not WIDE:
        return np.ones(k)
    levels = np.array([10, -10, 5, -5, 0])
    if k % 512:
        return np.exp2(np.random.permutation(np.resize(levels, k // 32))).repeat(32)
    a = np.empty((k // 512, 16))
    for p in range(k // 512):
        a[p, :8] = np.random.permutation(np.resize(levels, 8))
        for g in range(8):
            far = levels[np.abs(levels - a[p, g]) >= 10]
            a[p, g + 8] = far[np.random.randint(len(far))]
    return np.exp2(a.ravel()).repeat(32)


def f64(x):
    return np.asarray(x).astype(np.float64)


def striped8(idx):
    return np.asarray(idx).reshape(8, -1, 16).transpose(0, 2, 1).reshape(128, -1).astype(np.uint16)


def unstriped8(offs):
    return offs.reshape(8, 16, -1).transpose(0, 2, 1).reshape(8, -1).astype(np.int64)


def pick8(x, idx, run):
    r = np.arange(len(x))
    return x[r[:, None], idx[r % (8 * run) // run]]


E2M1 = np.array([0.0, 0.5, 1.0, 1.5, 2.0, 3.0, 4.0, 6.0, -0.0, -0.5, -1.0, -1.5, -2.0, -3.0, -4.0, -6.0])


def pack_weight(w, fmt):
    k, n = w.shape
    w = f64(np.asarray(w, np.float32).astype(ml_dtypes.bfloat16)).reshape(k // 32, 32, n)
    amax = np.abs(w).max(1)
    if fmt == "e4m3":
        byte = np.frexp(amax)[1] - 1 + 127 - 7
    else:
        mant, ex = np.frexp(amax / 6.0)
        byte = np.where(mant > 0.5, ex, ex - 1) + 127
    byte = np.clip(np.where(amax > 0, byte, 1), 1, 254)
    scaled = (w * np.exp2(127.0 - byte)[:, None, :]).reshape(k, n).astype(np.float32)
    by_word = np.ascontiguousarray(scaled.reshape(k // 512, 128, 4, n).transpose(0, 1, 3, 2))
    if fmt == "e4m3":
        words = by_word.astype(ml_dtypes.float8_e4m3fn).view(np.uint8)
    else:
        c = by_word.astype(ml_dtypes.float4_e2m1fn).view(np.uint8) & 0xF
        words = (c[..., 0::2] | (c[..., 1::2] << 4)).reshape(k // 512, 128, 2 * n)
    return np.ascontiguousarray(words), np.ascontiguousarray(byte.astype(np.uint8).reshape(k // 512, 16, n))


def unpack_weight(words, scales, fmt):
    g, _, n = scales.shape
    words = np.ascontiguousarray(words).reshape(g, 128, n, -1)
    if fmt == "e4m3":
        vals = words.view(ml_dtypes.float8_e4m3fn).astype(np.float64)
    else:
        nib = np.empty((g, 128, n, 4), np.uint8)
        nib[..., 0::2] = words & 0xF
        nib[..., 1::2] = words >> 4
        vals = E2M1[nib]
    vals = vals * np.repeat(np.exp2(scales.astype(np.float64) - 127.0), 8, axis=1)[..., None]
    return vals.transpose(0, 1, 3, 2).reshape(g * 512, n)


D, T, Q, I, V, E = 512, 1024, 128, 512, 1024, 512


def setup_inputs():
    n = np.random.standard_normal
    idx = np.stack([np.random.permutation(T)[:I] for _ in range(8)])
    idx2 = np.stack([np.random.permutation(T)[:I] for _ in range(8)])
    idx3 = np.stack([np.random.permutation(V)[:I] for _ in range(8)])
    fd = mx_kscale(D)
    fv = mx_kscale(V)
    keysp = pack_weight(n((D, T)) / fd[:, None], "e2m1")
    return {
        "query": (n((D, Q)) * 0.4 / np.sqrt(D) * fd[:, None]).astype(np.float32),
        "keys_words": keysp[0],
        "keys_scales": keysp[1],
        "fac": (np.random.uniform(4.0, 16.0, (1, V)) * fv).astype(np.float32),
        "vals": (n((V, E)) / fv[:, None]).astype(np.float32),
        "offs": striped8(idx),
        "offs2": striped8(idx2),
        "offs3": striped8(idx3),
    }


def reference(query, keys_words, keys_scales, fac, vals, offs, offs2, offs3):
    idx = unstriped8(offs)
    idx2 = unstriped8(offs2)
    idx3 = unstriped8(offs3)
    keysu = unpack_weight(keys_words, keys_scales, "e2m1")
    queryq = mxq(f64(query), 0, "e4m3")
    a = queryq.T @ keysu
    s = np.maximum(pick8(a, idx, 16), pick8(a, idx2, 16))
    p = np.exp(s - np.max(s, axis=1, keepdims=True))
    w = p / np.sum(p, axis=1, keepdims=True)
    wf = np.zeros((Q, V))
    wf[np.arange(Q)[:, None], idx3[np.arange(Q) % 128 // 16]] = w
    wg = wf * f64(fac)
    wt = wg.T
    wtq = mxq(wt, 0, "e4m3")
    valsq = mxq(f64(vals), 0, "e4m3")
    o = wtq.T @ valsq
    return o

@@ -1,0 +1,228 @@
+from contextlib import ExitStack
+
+import concourse.mybir as mybir
+from concourse.masks import make_identity
+
+D, T, Q, I, V, E = 512, 1024, 128, 512, 1024, 512
+FLOPS = 2 * D * Q * T + 2 * V * Q * E
+
+F32 = mybir.dt.float32
+BF16 = mybir.dt.bfloat16
+I32 = mybir.dt.int32
+U32 = mybir.dt.uint32
+U16 = mybir.dt.uint16
+U8 = mybir.dt.uint8
+FP8X4 = mybir.dt.float8_e4m3fn_x4
+FP4X4 = mybir.dt.float4_e2m1fn_x4
+ALU = mybir.AluOpType
+ACT = mybir.ActivationFunctionType
+AXIS = mybir.AxisListType
+
+P = 128
+PACK = 4
+K_PASS = P * PACK
+PASSES = V // K_PASS
+SCORE_N = 256
+OUT_N = 256
+
+
+def interleave(copy, grouped, raw):
+    copy(
+        out=grouped.rearrange("p (c i) t -> p c t i", i=4),
+        in_=raw.rearrange("p t (c i) -> p c t i", i=4),
+    )
+
+
+def tile_attend_twokeys_heads_kernel(tc, query, keys_words, keys_scales, fac, vals, offs, offs2, offs3, out):
+    nc = tc.nc
+    with ExitStack() as ctx:
+        keep = ctx.enter_context(tc.tile_pool(name="keep", bufs=1))
+        psum = ctx.enter_context(tc.psum_pool(name="psum", bufs=1))
+
+        k_scales = keep.tile([P, T], U8, name="k_scales", align_bytes=64)
+        nc.vector.memset(k_scales[:].bitcast(U32), 0)
+        warm_in = keep.tile([P, 1], F32, name="warm_in")
+        nc.vector.memset(warm_in[:], 0.0)
+        placed = keep.tile([P, V], F32, name="placed")
+        nc.vector.memset(placed[:], 0.0)
+        identity = keep.tile([P, P], F32, name="identity")
+        make_identity(nc, identity[:])
+
+        q_raw = keep.tile([P, PACK, Q], F32, name="q_raw")
+        nc.sync.dma_start(out=q_raw[:], in_=query.rearrange("(p j) q -> p j q", j=PACK))
+        k_words = keep.tile([P, 2 * T], U8, name="k_words", align_bytes=64)
+        nc.sync.dma_start(out=k_words[:].bitcast(I32), in_=keys_words[0].bitcast(I32))
+        for quad in range(4):
+            nc.scalar.dma_start(
+                out=k_scales[32 * quad : 32 * quad + 4, :].bitcast(I32),
+                in_=keys_scales[0, 4 * quad : 4 * quad + 4, :].bitcast(I32),
+            )
+        list1 = keep.tile([P, I // 16], U16, name="list1")
+        nc.sync.dma_start(out=list1[:], in_=offs)
+        list2 = keep.tile([P, I // 16], U16, name="list2")
+        nc.sync.dma_start(out=list2[:], in_=offs2)
+        v_raw = []
+        for g in range(PASSES):
+            v_raw.append(keep.tile([P, PACK, E], F32, name="v_raw%d" % g, tag="v_raw%d" % g))
+        nc.sync.dma_start(out=v_raw[0][:], in_=vals[0:K_PASS, :].rearrange("(p j) e -> p j e", j=PACK))
+        fac_cols = keep.tile([P, PASSES, PACK], F32, name="fac_cols")
+        nc.sync.dma_start(out=fac_cols[:], in_=fac[0].rearrange("(g p t) -> p g t", g=PASSES, t=PACK))
+        list3 = keep.tile([P, I // 16], U16, name="list3")
+        nc.sync.dma_start(out=list3[:], in_=offs3)
+        nc.sync.dma_start(out=v_raw[1][:], in_=vals[K_PASS:V, :].rearrange("(p j) e -> p j e", j=PACK))
+
+        warm_out = keep.tile([P, 1], F32, name="warm_out")
+        nc.scalar.activation(out=warm_out[:], in_=warm_in[:], func=ACT.Exp)
+
+        q_grouped = keep.tile([P, Q, PACK], BF16, name="q_grouped", align_bytes=64)
+        interleave(nc.vector.tensor_copy, q_grouped[:], q_raw[:])
+        q_codes = keep.tile([P, Q], U32, name="q_codes", align_bytes=64)
+        q_scales = keep.tile([P, Q], U8, name="q_scales", align_bytes=64)
+        nc.vector.quantize_mx(
+            out=q_codes[:].bitcast(FP8X4), scales=q_scales[:], in_=q_grouped[:].rearrange("p q t -> p (q t)")
+        )
+
+        scores = keep.tile([P, T], F32, name="scores")
+        for b in range(T // SCORE_N):
+            cols = slice(b * SCORE_N, (b + 1) * SCORE_N)
+            bank = psum.tile([P, SCORE_N], F32, name="score_bank%d" % b, tag="bank%d" % b)
+            nc.tensor.matmul_mx(
+                out=bank[:],
+                lhsT=q_codes[:].bitcast(FP8X4),
+                lhsT_scale=q_scales[:],
+                rhs=k_words[:, 2 * cols.start : 2 * cols.stop].bitcast(FP4X4),
+                rhs_scale=k_scales[:, cols],
+                start=True,
+                stop=True,
+            )
+            if b % 2 == 0:
+                nc.scalar.copy(out=scores[:, cols], in_=bank[:])
+            else:
+                nc.vector.tensor_copy(out=scores[:, cols], in_=bank[:])
+
+        fac_rows = []
+        for g in range(PASSES):
+            rows = psum.tile([P, PACK, P], F32, name="fac_rows%d" % g, tag="bank%d" % g)
+            for t in range(PACK):
+                nc.tensor.transpose(rows[:, t, :], fac_cols[:, g, t : t + 1].to_broadcast([P, P]), identity[:])
+            fac_rows.append(rows)
+
+        v_codes = []
+        v_scales = []
+        for g in range(PASSES):
+            v_codes.append(keep.tile([P, E], U32, name="v_codes%d" % g, align_bytes=64))
+            v_scales.append(keep.tile([P, E], U8, name="v_scales%d" % g, align_bytes=64))
+
+        def quantize_vals(g, cols, grouped):
+            nc.vector.quantize_mx(
+                out=v_codes[g][:, cols].bitcast(FP8X4),
+                scales=v_scales[g][:, cols],
+                in_=grouped[:].rearrange("p e t -> p (e t)"),
+            )
+
+        half = I // 2
+        lists = [slice(0, half // 16), slice(half // 16, I // 16)]
+        entries = [slice(0, half), slice(half, I)]
+        first = [keep.tile([P, half], F32, name="first%d" % c) for c in range(2)]
+        second = [keep.tile([P, half], F32, name="second%d" % c) for c in range(2)]
+        larger = [keep.tile([P, half], F32, name="larger%d" % c) for c in range(2)]
+        nc.vector.tensor_copy(first[0][:], scores[:].indirect(list1[:, lists[0]]))
+        nc.vector.tensor_copy(second[0][:], scores[:].indirect(list2[:, lists[0]]))
+        nc.vector.tensor_copy(first[1][:], scores[:].indirect(list1[:, lists[1]]))
+        nc.vector.tensor_tensor(out=larger[0][:], in0=first[0][:], in1=second[0][:], op=ALU.max)
+        nc.vector.tensor_copy(second[1][:], scores[:].indirect(list2[:, lists[1]]))
+        neg_max0 = keep.tile([P, 1], F32, name="neg_max0")
+        nc.vector.tensor_reduce(out=neg_max0[:], in_=larger[0][:], axis=AXIS.X, op=ALU.max, negate=True)
+        nc.vector.tensor_tensor(out=larger[1][:], in0=first[1][:], in1=second[1][:], op=ALU.max)
+        neg_larger1 = keep.tile([P, half], F32, name="neg_larger1")
+        neg_max = keep.tile([P, 1], F32, name="neg_max")
+        nc.vector.tensor_scalar(
+            out=neg_larger1[:],
+            in0=larger[1][:],
+            scalar1=-1.0,
+            scalar2=neg_max0[:],
+            op0=ALU.mult,
+            op1=ALU.min,
+            accum_out=neg_max[:],
+        )
+
+        v_grouped0 = keep.tile([P, E, PACK], BF16, name="v_grouped0", align_bytes=64)
+        interleave(nc.scalar.copy, v_grouped0[:], v_raw[0][:])
+        quantize_vals(0, slice(0, E), v_grouped0)
+
+        weights = keep.tile([P, I], F32, name="weights", tag="v_raw0")
+        sum0 = keep.tile([P, 1], F32, name="sum0")
+        sum1 = keep.tile([P, 1], F32, name="sum1")
+        nc.scalar.activation(
+            out=weights[:, entries[0]], in_=larger[0][:], func=ACT.Exp, bias=neg_max[:], accum_out=sum0[:]
+        )
+        nc.scalar.activation(
+            out=weights[:, entries[1]],
+            in_=neg_larger1[:],
+            func=ACT.Exp,
+            scale=-1.0,
+            bias=neg_max[:],
+            accum_out=sum1[:],
+        )
+        row_sum = keep.tile([P, 1], F32, name="row_sum")
+        nc.scalar.activation(out=row_sum[:], in_=sum0[:], func=ACT.Identity, bias=sum1[:])
+        v_grouped1 = []
+        for h in range(E // OUT_N):
+            grouped = keep.tile([P, OUT_N, PACK], BF16, name="v_grouped1_%d" % h, tag="late%d" % h, align_bytes=64)
+            interleave(nc.scalar.copy, grouped[:], v_raw[1][:, :, h * OUT_N : (h + 1) * OUT_N])
+            v_grouped1.append(grouped)
+
+        nc.vector.tensor_copy(placed[:].indirect(list3[:, lists[0]]), weights[:, entries[0]])
+        inv_sum = keep.tile([P, 1], F32, name="inv_sum")
+        nc.vector.reciprocal(out=inv_sum[:], in_=row_sum[:])
+        nc.vector.tensor_copy(placed[:].indirect(list3[:, lists[1]]), weights[:, entries[1]])
+
+        w_grouped = []
+        for g in range(PASSES):
+            scaled = keep.tile([P, P, PACK], BF16, name="scaled%d" % g)
+            nc.vector.scalar_tensor_tensor(
+                out=scaled[:],
+                in0=placed[:, g * K_PASS : (g + 1) * K_PASS].rearrange("q (p t) -> q p t", t=PACK),
+                scalar=inv_sum[:],
+                in1=fac_rows[g][:].rearrange("q t p -> q p t"),
+                op0=ALU.mult,
+                op1=ALU.mult,
+            )
+            words = scaled[:].rearrange("q p t -> q (p t)").bitcast(F32)
+            turned = psum.tile([P, 2, Q], F32, name="turned%d" % g, tag="bank%d" % (2 + g))
+            for u in range(2):
+                nc.tensor.transpose(turned[:, u, :], words[:, u : 2 * P : 2], identity[:])
+            grouped = keep.tile([P, Q, PACK], BF16, name="w_grouped%d" % g, align_bytes=64)
+            nc.scalar.copy(out=grouped[:].bitcast(F32), in_=turned[:].rearrange("p u q -> p q u"))
+            w_grouped.append(grouped)
+
+        out_banks = []
+        for h in range(E // OUT_N):
+            out_banks.append(psum.tile([P, OUT_N], F32, name="out_bank%d" % h))
+        for g in range(PASSES):
+            quantize_vals(1, slice(g * OUT_N, (g + 1) * OUT_N), v_grouped1[g])
+            w_codes = keep.tile([P, Q], U32, name="w_codes%d" % g, tag="late%d" % g, align_bytes=64)
+            w_scales = keep.tile([P, Q], U8, name="w_scales%d" % g, align_bytes=64)
+            nc.vector.quantize_mx(
+                out=w_codes[:].bitcast(FP8X4), scales=w_scales[:], in_=w_grouped[g][:].rearrange("p q t -> p (q t)")
+            )
+            for h in range(E // OUT_N):
+                cols = slice(h * OUT_N, (h + 1) * OUT_N)
+                nc.tensor.matmul_mx(
+                    out=out_banks[h][:],
+                    lhsT=w_codes[:].bitcast(FP8X4),
+                    lhsT_scale=w_scales[:],
+                    rhs=v_codes[g][:, cols].bitcast(FP8X4),
+                    rhs_scale=v_scales[g][:, cols],
+                    start=(g == 0),
+                    stop=(g == PASSES - 1),
+                )
+        for h in range(E // OUT_N):
+            cols = slice(h * OUT_N, (h + 1) * OUT_N)
+            result = keep.tile([P, OUT_N], F32, name="result%d" % h)
+            if h == 0:
+                nc.scalar.copy(out=result[:], in_=out_banks[h][:])
+                nc.scalar.dma_start(out=out[:, cols], in_=result[:])
+            else:
+                nc.vector.tensor_copy(out=result[:], in_=out_banks[h][:])
+                nc.sync.dma_start(out=out[:, cols], in_=result[:])

@@ -22,8 +22,9 @@ P = 128
 PACK = 4
 K_PASS = P * PACK
 PASSES = V // K_PASS
-SCORE_N = 256
-OUT_N = 256
+SCORE_SPLIT = (512, 256, 128, 128)
+OUT_SPLIT = (256, 128, 128)
+HALF_E = E // 2
 
 
 def interleave(copy, grouped, raw):
@@ -31,6 +32,10 @@ def interleave(copy, grouped, raw):
         out=grouped.rearrange("p (c i) t -> p c t i", i=4),
         in_=raw.rearrange("p t (c i) -> p c t i", i=4),
     )
+
+
+def runs(widths):
+    return [slice(sum(widths[:n]), sum(widths[: n + 1])) for n in range(len(widths))]
 
 
 def tile_attend_twokeys_heads_kernel(tc, query, keys_words, keys_scales, fac, vals, offs, offs2, offs3, out):
@@ -53,18 +58,18 @@ def tile_attend_twokeys_heads_kernel(tc, query, keys_words, keys_scales, fac, va
         k_words = keep.tile([P, 2 * T], U8, name="k_words", align_bytes=64)
         nc.sync.dma_start(out=k_words[:].bitcast(I32), in_=keys_words[0].bitcast(I32))
         for quad in range(4):
-            nc.scalar.dma_start(
+            nc.sync.dma_start(
                 out=k_scales[32 * quad : 32 * quad + 4, :].bitcast(I32),
                 in_=keys_scales[0, 4 * quad : 4 * quad + 4, :].bitcast(I32),
             )
         list1 = keep.tile([P, I // 16], U16, name="list1")
         nc.sync.dma_start(out=list1[:], in_=offs)
-        list2 = keep.tile([P, I // 16], U16, name="list2")
-        nc.sync.dma_start(out=list2[:], in_=offs2)
         v_raw = []
         for g in range(PASSES):
             v_raw.append(keep.tile([P, PACK, E], F32, name="v_raw%d" % g, tag="v_raw%d" % g))
         nc.sync.dma_start(out=v_raw[0][:], in_=vals[0:K_PASS, :].rearrange("(p j) e -> p j e", j=PACK))
+        list2 = keep.tile([P, I // 16], U16, name="list2")
+        nc.sync.dma_start(out=list2[:], in_=offs2)
         fac_cols = keep.tile([P, PASSES, PACK], F32, name="fac_cols")
         nc.sync.dma_start(out=fac_cols[:], in_=fac[0].rearrange("(g p t) -> p g t", g=PASSES, t=PACK))
         list3 = keep.tile([P, I // 16], U16, name="list3")
@@ -83,9 +88,8 @@ def tile_attend_twokeys_heads_kernel(tc, query, keys_words, keys_scales, fac, va
         )
 
         scores = keep.tile([P, T], F32, name="scores")
-        for b in range(T // SCORE_N):
-            cols = slice(b * SCORE_N, (b + 1) * SCORE_N)
-            bank = psum.tile([P, SCORE_N], F32, name="score_bank%d" % b, tag="bank%d" % b)
+        for b, cols in enumerate(runs(SCORE_SPLIT)):
+            bank = psum.tile([P, SCORE_SPLIT[b]], F32, name="score_bank%d" % b, tag="bank%d" % b)
             nc.tensor.matmul_mx(
                 out=bank[:],
                 lhsT=q_codes[:].bitcast(FP8X4),
@@ -167,9 +171,9 @@ def tile_attend_twokeys_heads_kernel(tc, query, keys_words, keys_scales, fac, va
         row_sum = keep.tile([P, 1], F32, name="row_sum")
         nc.scalar.activation(out=row_sum[:], in_=sum0[:], func=ACT.Identity, bias=sum1[:])
         v_grouped1 = []
-        for h in range(E // OUT_N):
-            grouped = keep.tile([P, OUT_N, PACK], BF16, name="v_grouped1_%d" % h, tag="late%d" % h, align_bytes=64)
-            interleave(nc.scalar.copy, grouped[:], v_raw[1][:, :, h * OUT_N : (h + 1) * OUT_N])
+        for h in range(2):
+            grouped = keep.tile([P, HALF_E, PACK], BF16, name="v_grouped1_%d" % h, tag="late%d" % h, align_bytes=64)
+            interleave(nc.scalar.copy, grouped[:], v_raw[1][:, :, h * HALF_E : (h + 1) * HALF_E])
             v_grouped1.append(grouped)
 
         nc.vector.tensor_copy(placed[:].indirect(list3[:, lists[0]]), weights[:, entries[0]])
@@ -179,35 +183,33 @@ def tile_attend_twokeys_heads_kernel(tc, query, keys_words, keys_scales, fac, va
 
         w_grouped = []
         for g in range(PASSES):
-            scaled = keep.tile([P, P, PACK], BF16, name="scaled%d" % g)
-            nc.vector.scalar_tensor_tensor(
-                out=scaled[:],
-                in0=placed[:, g * K_PASS : (g + 1) * K_PASS].rearrange("q (p t) -> q p t", t=PACK),
-                scalar=inv_sum[:],
-                in1=fac_rows[g][:].rearrange("q t p -> q p t"),
-                op0=ALU.mult,
-                op1=ALU.mult,
-            )
-            words = scaled[:].rearrange("q p t -> q (p t)").bitcast(F32)
             turned = psum.tile([P, 2, Q], F32, name="turned%d" % g, tag="bank%d" % (2 + g))
             for u in range(2):
-                nc.tensor.transpose(turned[:, u, :], words[:, u : 2 * P : 2], identity[:])
+                scaled = keep.tile([P, P, 2], BF16, name="scaled%d_%d" % (g, u))
+                nc.vector.scalar_tensor_tensor(
+                    out=scaled[:],
+                    in0=placed[:, g * K_PASS : (g + 1) * K_PASS].rearrange("q (p t) -> q p t", t=PACK)[:, :, 2 * u : 2 * u + 2],
+                    scalar=inv_sum[:],
+                    in1=fac_rows[g][:, 2 * u : 2 * u + 2, :].rearrange("q t p -> q p t"),
+                    op0=ALU.mult,
+                    op1=ALU.mult,
+                )
+                nc.tensor.transpose(turned[:, u, :], scaled[:].rearrange("q p t -> q (p t)").bitcast(F32), identity[:])
             grouped = keep.tile([P, Q, PACK], BF16, name="w_grouped%d" % g, align_bytes=64)
             nc.scalar.copy(out=grouped[:].bitcast(F32), in_=turned[:].rearrange("p u q -> p q u"))
             w_grouped.append(grouped)
 
         out_banks = []
-        for h in range(E // OUT_N):
-            out_banks.append(psum.tile([P, OUT_N], F32, name="out_bank%d" % h))
+        for h, width in enumerate(OUT_SPLIT):
+            out_banks.append(psum.tile([P, width], F32, name="out_bank%d" % h))
         for g in range(PASSES):
-            quantize_vals(1, slice(g * OUT_N, (g + 1) * OUT_N), v_grouped1[g])
+            quantize_vals(1, slice(g * HALF_E, (g + 1) * HALF_E), v_grouped1[g])
             w_codes = keep.tile([P, Q], U32, name="w_codes%d" % g, tag="late%d" % g, align_bytes=64)
             w_scales = keep.tile([P, Q], U8, name="w_scales%d" % g, align_bytes=64)
             nc.vector.quantize_mx(
                 out=w_codes[:].bitcast(FP8X4), scales=w_scales[:], in_=w_grouped[g][:].rearrange("p q t -> p (q t)")
             )
-            for h in range(E // OUT_N):
-                cols = slice(h * OUT_N, (h + 1) * OUT_N)
+            for h, cols in enumerate(runs(OUT_SPLIT)):
                 nc.tensor.matmul_mx(
                     out=out_banks[h][:],
                     lhsT=w_codes[:].bitcast(FP8X4),
@@ -217,9 +219,8 @@ def tile_attend_twokeys_heads_kernel(tc, query, keys_words, keys_scales, fac, va
                     start=(g == 0),
                     stop=(g == PASSES - 1),
                 )
-        for h in range(E // OUT_N):
-            cols = slice(h * OUT_N, (h + 1) * OUT_N)
-            result = keep.tile([P, OUT_N], F32, name="result%d" % h)
+        for h, cols in enumerate(runs(OUT_SPLIT)):
+            result = keep.tile([P, OUT_SPLIT[h]], F32, name="result%d" % h)
             if h == 0:
                 nc.scalar.copy(out=result[:], in_=out_banks[h][:])
                 nc.scalar.dma_start(out=out[:, cols], in_=result[:])

@@ -25,6 +25,9 @@ PASSES = V // K_PASS
 SCORE_SPLIT = (512, 256, 128, 128)
 OUT_SPLIT = (256, 128, 128)
 HALF_E = E // 2
+Q_ON_VECTOR = 80
+GATHER_SPLIT = (256, 256)
+EXP_SPLIT = (192, 320)
 
 
 def interleave(copy, grouped, raw):
@@ -48,19 +51,20 @@ def tile_attend_twokeys_heads_kernel(tc, query, keys_words, keys_scales, fac, va
         nc.vector.memset(k_scales[:].bitcast(U32), 0)
         warm_in = keep.tile([P, 1], F32, name="warm_in")
         nc.vector.memset(warm_in[:], 0.0)
+        identity = keep.tile([P, P], F32, name="identity")
+        nc.vector.memset(identity[:], 0.0)
+        make_identity(nc, identity[:], nomemset=True)
         placed = keep.tile([P, V], F32, name="placed")
         nc.vector.memset(placed[:], 0.0)
-        identity = keep.tile([P, P], F32, name="identity")
-        make_identity(nc, identity[:])
 
         q_raw = keep.tile([P, PACK, Q], F32, name="q_raw")
         nc.sync.dma_start(out=q_raw[:], in_=query.rearrange("(p j) q -> p j q", j=PACK))
         k_words = keep.tile([P, 2 * T], U8, name="k_words", align_bytes=64)
         nc.sync.dma_start(out=k_words[:].bitcast(I32), in_=keys_words[0].bitcast(I32))
-        for quad in range(4):
+        for row in range(4):
             nc.sync.dma_start(
-                out=k_scales[32 * quad : 32 * quad + 4, :].bitcast(I32),
-                in_=keys_scales[0, 4 * quad : 4 * quad + 4, :].bitcast(I32),
+                out=k_scales[row:P:32, :].bitcast(I32),
+                in_=keys_scales[0, row:16:4, :].bitcast(I32),
             )
         list1 = keep.tile([P, I // 16], U16, name="list1")
         nc.sync.dma_start(out=list1[:], in_=offs)
@@ -80,7 +84,8 @@ def tile_attend_twokeys_heads_kernel(tc, query, keys_words, keys_scales, fac, va
         nc.scalar.activation(out=warm_out[:], in_=warm_in[:], func=ACT.Exp)
 
         q_grouped = keep.tile([P, Q, PACK], BF16, name="q_grouped", align_bytes=64)
-        interleave(nc.vector.tensor_copy, q_grouped[:], q_raw[:])
+        interleave(nc.vector.tensor_copy, q_grouped[:, 0:Q_ON_VECTOR, :], q_raw[:, :, 0:Q_ON_VECTOR])
+        interleave(nc.scalar.copy, q_grouped[:, Q_ON_VECTOR:Q, :], q_raw[:, :, Q_ON_VECTOR:Q])
         q_codes = keep.tile([P, Q], U32, name="q_codes", align_bytes=64)
         q_scales = keep.tile([P, Q], U8, name="q_scales", align_bytes=64)
         nc.vector.quantize_mx(
@@ -124,62 +129,42 @@ def tile_attend_twokeys_heads_kernel(tc, query, keys_words, keys_scales, fac, va
                 in_=grouped[:].rearrange("p e t -> p (e t)"),
             )
 
-        half = I // 2
-        lists = [slice(0, half // 16), slice(half // 16, I // 16)]
-        entries = [slice(0, half), slice(half, I)]
-        first = [keep.tile([P, half], F32, name="first%d" % c) for c in range(2)]
-        second = [keep.tile([P, half], F32, name="second%d" % c) for c in range(2)]
-        larger = [keep.tile([P, half], F32, name="larger%d" % c) for c in range(2)]
-        nc.vector.tensor_copy(first[0][:], scores[:].indirect(list1[:, lists[0]]))
-        nc.vector.tensor_copy(second[0][:], scores[:].indirect(list2[:, lists[0]]))
-        nc.vector.tensor_copy(first[1][:], scores[:].indirect(list1[:, lists[1]]))
-        nc.vector.tensor_tensor(out=larger[0][:], in0=first[0][:], in1=second[0][:], op=ALU.max)
-        nc.vector.tensor_copy(second[1][:], scores[:].indirect(list2[:, lists[1]]))
-        neg_max0 = keep.tile([P, 1], F32, name="neg_max0")
-        nc.vector.tensor_reduce(out=neg_max0[:], in_=larger[0][:], axis=AXIS.X, op=ALU.max, negate=True)
-        nc.vector.tensor_tensor(out=larger[1][:], in0=first[1][:], in1=second[1][:], op=ALU.max)
-        neg_larger1 = keep.tile([P, half], F32, name="neg_larger1")
+        first = keep.tile([P, I], F32, name="first")
+        nc.vector.tensor_copy(first[:], scores[:].indirect(list1[:]))
+        second = []
+        for c, entries in enumerate(runs(GATHER_SPLIT)):
+            second.append(keep.tile([P, GATHER_SPLIT[c]], F32, name="second%d" % c))
+            nc.vector.tensor_copy(second[c][:], scores[:].indirect(list2[:, entries.start // 16 : entries.stop // 16]))
+        larger = keep.tile([P, I], F32, name="larger")
+        for c, entries in enumerate(runs(GATHER_SPLIT)):
+            nc.vector.tensor_tensor(out=larger[:, entries], in0=first[:, entries], in1=second[c][:], op=ALU.max)
         neg_max = keep.tile([P, 1], F32, name="neg_max")
-        nc.vector.tensor_scalar(
-            out=neg_larger1[:],
-            in0=larger[1][:],
-            scalar1=-1.0,
-            scalar2=neg_max0[:],
-            op0=ALU.mult,
-            op1=ALU.min,
-            accum_out=neg_max[:],
-        )
+        nc.vector.tensor_reduce(out=neg_max[:], in_=larger[:], axis=AXIS.X, op=ALU.max, negate=True)
 
         v_grouped0 = keep.tile([P, E, PACK], BF16, name="v_grouped0", align_bytes=64)
         interleave(nc.scalar.copy, v_grouped0[:], v_raw[0][:])
         quantize_vals(0, slice(0, E), v_grouped0)
 
         weights = keep.tile([P, I], F32, name="weights", tag="v_raw0")
-        sum0 = keep.tile([P, 1], F32, name="sum0")
-        sum1 = keep.tile([P, 1], F32, name="sum1")
-        nc.scalar.activation(
-            out=weights[:, entries[0]], in_=larger[0][:], func=ACT.Exp, bias=neg_max[:], accum_out=sum0[:]
-        )
-        nc.scalar.activation(
-            out=weights[:, entries[1]],
-            in_=neg_larger1[:],
-            func=ACT.Exp,
-            scale=-1.0,
-            bias=neg_max[:],
-            accum_out=sum1[:],
-        )
+        sums = []
+        for c, entries in enumerate(runs(EXP_SPLIT)):
+            sums.append(keep.tile([P, 1], F32, name="sum%d" % c))
+            nc.scalar.activation(
+                out=weights[:, entries], in_=larger[:, entries], func=ACT.Exp, bias=neg_max[:], accum_out=sums[c][:]
+            )
         row_sum = keep.tile([P, 1], F32, name="row_sum")
-        nc.scalar.activation(out=row_sum[:], in_=sum0[:], func=ACT.Identity, bias=sum1[:])
+        nc.scalar.activation(out=row_sum[:], in_=sums[0][:], func=ACT.Identity, bias=sums[1][:])
         v_grouped1 = []
         for h in range(2):
             grouped = keep.tile([P, HALF_E, PACK], BF16, name="v_grouped1_%d" % h, tag="late%d" % h, align_bytes=64)
             interleave(nc.scalar.copy, grouped[:], v_raw[1][:, :, h * HALF_E : (h + 1) * HALF_E])
             v_grouped1.append(grouped)
 
-        nc.vector.tensor_copy(placed[:].indirect(list3[:, lists[0]]), weights[:, entries[0]])
+        early, late = runs(EXP_SPLIT)
+        nc.vector.tensor_copy(placed[:].indirect(list3[:, early.start // 16 : early.stop // 16]), weights[:, early])
         inv_sum = keep.tile([P, 1], F32, name="inv_sum")
         nc.vector.reciprocal(out=inv_sum[:], in_=row_sum[:])
-        nc.vector.tensor_copy(placed[:].indirect(list3[:, lists[1]]), weights[:, entries[1]])
+        nc.vector.tensor_copy(placed[:].indirect(list3[:, late.start // 16 : late.stop // 16]), weights[:, late])
 
         w_grouped = []
         for g in range(PASSES):
@@ -204,7 +189,7 @@ def tile_attend_twokeys_heads_kernel(tc, query, keys_words, keys_scales, fac, va
             out_banks.append(psum.tile([P, width], F32, name="out_bank%d" % h))
         for g in range(PASSES):
             quantize_vals(1, slice(g * HALF_E, (g + 1) * HALF_E), v_grouped1[g])
-            w_codes = keep.tile([P, Q], U32, name="w_codes%d" % g, tag="late%d" % g, align_bytes=64)
+            w_codes = keep.tile([P, Q], U32, name="w_codes%d" % g, tag="late0" if g == 0 else "w_codes1", align_bytes=64)
             w_scales = keep.tile([P, Q], U8, name="w_scales%d" % g, align_bytes=64)
             nc.vector.quantize_mx(
                 out=w_codes[:].bitcast(FP8X4), scales=w_scales[:], in_=w_grouped[g][:].rearrange("p q t -> p (q t)")

from contextlib import ExitStack

import concourse.mybir as mybir
from concourse.masks import make_identity

D, T, Q, I, V, E = 512, 1024, 128, 512, 1024, 512
FLOPS = 2 * D * Q * T + 2 * V * Q * E

F32 = mybir.dt.float32
BF16 = mybir.dt.bfloat16
I32 = mybir.dt.int32
U32 = mybir.dt.uint32
U16 = mybir.dt.uint16
U8 = mybir.dt.uint8
FP8X4 = mybir.dt.float8_e4m3fn_x4
FP4X4 = mybir.dt.float4_e2m1fn_x4
ALU = mybir.AluOpType
ACT = mybir.ActivationFunctionType
AXIS = mybir.AxisListType

P = 128
PACK = 4
K_PASS = P * PACK
PASSES = V // K_PASS
SCORE_SPLIT = (512, 256, 128, 128)
OUT_SPLIT = (256, 128, 128)
HALF_E = E // 2
Q_ON_VECTOR = 80
GATHER_SPLIT = (256, 256)
EXP_SPLIT = (192, 320)


def interleave(copy, grouped, raw):
    copy(
        out=grouped.rearrange("p (c i) t -> p c t i", i=4),
        in_=raw.rearrange("p t (c i) -> p c t i", i=4),
    )


def runs(widths):
    return [slice(sum(widths[:n]), sum(widths[: n + 1])) for n in range(len(widths))]


def tile_attend_twokeys_heads_kernel(tc, query, keys_words, keys_scales, fac, vals, offs, offs2, offs3, out):
    nc = tc.nc
    with ExitStack() as ctx:
        keep = ctx.enter_context(tc.tile_pool(name="keep", bufs=1))
        psum = ctx.enter_context(tc.psum_pool(name="psum", bufs=1))

        k_scales = keep.tile([P, T], U8, name="k_scales", align_bytes=64)
        nc.vector.memset(k_scales[:].bitcast(U32), 0)
        warm_in = keep.tile([P, 1], F32, name="warm_in")
        nc.vector.memset(warm_in[:], 0.0)
        identity = keep.tile([P, P], F32, name="identity")
        nc.vector.memset(identity[:], 0.0)
        make_identity(nc, identity[:], nomemset=True)
        placed = keep.tile([P, V], F32, name="placed")
        nc.vector.memset(placed[:], 0.0)

        q_raw = keep.tile([P, PACK, Q], F32, name="q_raw")
        nc.sync.dma_start(out=q_raw[:], in_=query.rearrange("(p j) q -> p j q", j=PACK))
        k_words = keep.tile([P, 2 * T], U8, name="k_words", align_bytes=64)
        nc.sync.dma_start(out=k_words[:].bitcast(I32), in_=keys_words[0].bitcast(I32))
        for row in range(4):
            nc.sync.dma_start(
                out=k_scales[row:P:32, :].bitcast(I32),
                in_=keys_scales[0, row:16:4, :].bitcast(I32),
            )
        list1 = keep.tile([P, I // 16], U16, name="list1")
        nc.sync.dma_start(out=list1[:], in_=offs)
        v_raw = []
        for g in range(PASSES):
            v_raw.append(keep.tile([P, PACK, E], F32, name="v_raw%d" % g, tag="v_raw%d" % g))
        nc.sync.dma_start(out=v_raw[0][:], in_=vals[0:K_PASS, :].rearrange("(p j) e -> p j e", j=PACK))
        list2 = keep.tile([P, I // 16], U16, name="list2")
        nc.sync.dma_start(out=list2[:], in_=offs2)
        fac_cols = keep.tile([P, PASSES, PACK], F32, name="fac_cols")
        nc.sync.dma_start(out=fac_cols[:], in_=fac[0].rearrange("(g p t) -> p g t", g=PASSES, t=PACK))
        list3 = keep.tile([P, I // 16], U16, name="list3")
        nc.sync.dma_start(out=list3[:], in_=offs3)
        nc.sync.dma_start(out=v_raw[1][:], in_=vals[K_PASS:V, :].rearrange("(p j) e -> p j e", j=PACK))

        warm_out = keep.tile([P, 1], F32, name="warm_out")
        nc.scalar.activation(out=warm_out[:], in_=warm_in[:], func=ACT.Exp)

        q_grouped = keep.tile([P, Q, PACK], BF16, name="q_grouped", align_bytes=64)
        interleave(nc.vector.tensor_copy, q_grouped[:, 0:Q_ON_VECTOR, :], q_raw[:, :, 0:Q_ON_VECTOR])
        interleave(nc.scalar.copy, q_grouped[:, Q_ON_VECTOR:Q, :], q_raw[:, :, Q_ON_VECTOR:Q])
        q_codes = keep.tile([P, Q], U32, name="q_codes", align_bytes=64)
        q_scales = keep.tile([P, Q], U8, name="q_scales", align_bytes=64)
        nc.vector.quantize_mx(
            out=q_codes[:].bitcast(FP8X4), scales=q_scales[:], in_=q_grouped[:].rearrange("p q t -> p (q t)")
        )

        scores = keep.tile([P, T], F32, name="scores")
        for b, cols in enumerate(runs(SCORE_SPLIT)):
            bank = psum.tile([P, SCORE_SPLIT[b]], F32, name="score_bank%d" % b, tag="bank%d" % b)
            nc.tensor.matmul_mx(
                out=bank[:],
                lhsT=q_codes[:].bitcast(FP8X4),
                lhsT_scale=q_scales[:],
                rhs=k_words[:, 2 * cols.start : 2 * cols.stop].bitcast(FP4X4),
                rhs_scale=k_scales[:, cols],
                start=True,
                stop=True,
            )
            if b % 2 == 0:
                nc.scalar.copy(out=scores[:, cols], in_=bank[:])
            else:
                nc.vector.tensor_copy(out=scores[:, cols], in_=bank[:])

        fac_rows = []
        for g in range(PASSES):
            rows = psum.tile([P, PACK, P], F32, name="fac_rows%d" % g, tag="bank%d" % g)
            for t in range(PACK):
                nc.tensor.transpose(rows[:, t, :], fac_cols[:, g, t : t + 1].to_broadcast([P, P]), identity[:])
            fac_rows.append(rows)

        v_codes = []
        v_scales = []
        for g in range(PASSES):
            v_codes.append(keep.tile([P, E], U32, name="v_codes%d" % g, align_bytes=64))
            v_scales.append(keep.tile([P, E], U8, name="v_scales%d" % g, align_bytes=64))

        def quantize_vals(g, cols, grouped):
            nc.vector.quantize_mx(
                out=v_codes[g][:, cols].bitcast(FP8X4),
                scales=v_scales[g][:, cols],
                in_=grouped[:].rearrange("p e t -> p (e t)"),
            )

        first = keep.tile([P, I], F32, name="first")
        nc.vector.tensor_copy(first[:], scores[:].indirect(list1[:]))
        second = []
        for c, entries in enumerate(runs(GATHER_SPLIT)):
            second.append(keep.tile([P, GATHER_SPLIT[c]], F32, name="second%d" % c))
            nc.vector.tensor_copy(second[c][:], scores[:].indirect(list2[:, entries.start // 16 : entries.stop // 16]))
        larger = keep.tile([P, I], F32, name="larger")
        for c, entries in enumerate(runs(GATHER_SPLIT)):
            nc.vector.tensor_tensor(out=larger[:, entries], in0=first[:, entries], in1=second[c][:], op=ALU.max)
        neg_max = keep.tile([P, 1], F32, name="neg_max")
        nc.vector.tensor_reduce(out=neg_max[:], in_=larger[:], axis=AXIS.X, op=ALU.max, negate=True)

        v_grouped0 = keep.tile([P, E, PACK], BF16, name="v_grouped0", align_bytes=64)
        interleave(nc.scalar.copy, v_grouped0[:], v_raw[0][:])
        quantize_vals(0, slice(0, E), v_grouped0)

        weights = keep.tile([P, I], F32, name="weights", tag="v_raw0")
        sums = []
        for c, entries in enumerate(runs(EXP_SPLIT)):
            sums.append(keep.tile([P, 1], F32, name="sum%d" % c))
            nc.scalar.activation(
                out=weights[:, entries], in_=larger[:, entries], func=ACT.Exp, bias=neg_max[:], accum_out=sums[c][:]
            )
        row_sum = keep.tile([P, 1], F32, name="row_sum")
        nc.scalar.activation(out=row_sum[:], in_=sums[0][:], func=ACT.Identity, bias=sums[1][:])
        v_grouped1 = []
        for h in range(2):
            grouped = keep.tile([P, HALF_E, PACK], BF16, name="v_grouped1_%d" % h, tag="late%d" % h, align_bytes=64)
            interleave(nc.scalar.copy, grouped[:], v_raw[1][:, :, h * HALF_E : (h + 1) * HALF_E])
            v_grouped1.append(grouped)

        early, late = runs(EXP_SPLIT)
        nc.vector.tensor_copy(placed[:].indirect(list3[:, early.start // 16 : early.stop // 16]), weights[:, early])
        inv_sum = keep.tile([P, 1], F32, name="inv_sum")
        nc.vector.reciprocal(out=inv_sum[:], in_=row_sum[:])
        nc.vector.tensor_copy(placed[:].indirect(list3[:, late.start // 16 : late.stop // 16]), weights[:, late])

        w_grouped = []
        for g in range(PASSES):
            turned = psum.tile([P, 2, Q], F32, name="turned%d" % g, tag="bank%d" % (2 + g))
            for u in range(2):
                scaled = keep.tile([P, P, 2], BF16, name="scaled%d_%d" % (g, u))
                nc.vector.scalar_tensor_tensor(
                    out=scaled[:],
                    in0=placed[:, g * K_PASS : (g + 1) * K_PASS].rearrange("q (p t) -> q p t", t=PACK)[:, :, 2 * u : 2 * u + 2],
                    scalar=inv_sum[:],
                    in1=fac_rows[g][:, 2 * u : 2 * u + 2, :].rearrange("q t p -> q p t"),
                    op0=ALU.mult,
                    op1=ALU.mult,
                )
                nc.tensor.transpose(turned[:, u, :], scaled[:].rearrange("q p t -> q (p t)").bitcast(F32), identity[:])
            grouped = keep.tile([P, Q, PACK], BF16, name="w_grouped%d" % g, align_bytes=64)
            nc.scalar.copy(out=grouped[:].bitcast(F32), in_=turned[:].rearrange("p u q -> p q u"))
            w_grouped.append(grouped)

        out_banks = []
        for h, width in enumerate(OUT_SPLIT):
            out_banks.append(psum.tile([P, width], F32, name="out_bank%d" % h))
        for g in range(PASSES):
            quantize_vals(1, slice(g * HALF_E, (g + 1) * HALF_E), v_grouped1[g])
            w_codes = keep.tile([P, Q], U32, name="w_codes%d" % g, tag="late0" if g == 0 else "w_codes1", align_bytes=64)
            w_scales = keep.tile([P, Q], U8, name="w_scales%d" % g, align_bytes=64)
            nc.vector.quantize_mx(
                out=w_codes[:].bitcast(FP8X4), scales=w_scales[:], in_=w_grouped[g][:].rearrange("p q t -> p (q t)")
            )
            for h, cols in enumerate(runs(OUT_SPLIT)):
                nc.tensor.matmul_mx(
                    out=out_banks[h][:],
                    lhsT=w_codes[:].bitcast(FP8X4),
                    lhsT_scale=w_scales[:],
                    rhs=v_codes[g][:, cols].bitcast(FP8X4),
                    rhs_scale=v_scales[g][:, cols],
                    start=(g == 0),
                    stop=(g == PASSES - 1),
                )
        for h, cols in enumerate(runs(OUT_SPLIT)):
            result = keep.tile([P, OUT_SPLIT[h]], F32, name="result%d" % h)
            if h == 0:
                nc.scalar.copy(out=result[:], in_=out_banks[h][:])
                nc.scalar.dma_start(out=out[:, cols], in_=result[:])
            else:
                nc.vector.tensor_copy(out=result[:], in_=out_banks[h][:])
                nc.sync.dma_start(out=out[:, cols], in_=result[:])
